import numpy as np, ml_dtypes
CORES = [16,18,20,22]
N = 4
import mx_ref
BF = ml_dtypes.bfloat16
def entries(a):
    return np.ascontiguousarray(a.T).reshape(-1)
def table(e):
    return np.ascontiguousarray(np.reshape(e, (-1, 16)).T).astype(np.int32)
def pick(q, e):
    c = np.concatenate([q[0].reshape(128, -1, 4), np.zeros((128, 1, 4), np.uint8)], axis=1); s = np.concatenate([q[1], np.ones((16, 1), np.uint8)], axis=1)
    return (np.ascontiguousarray(c[:, e].reshape(128, -1)), np.ascontiguousarray(s[:, e]))
def join(*qs):
    return (np.concatenate([q[0] for q in qs], axis=1), np.concatenate([q[1] for q in qs], axis=1))
def put(q, e, v):
    c, s = q[0].reshape(128, -1, 4).copy(), q[1].copy(); c[:, e] = v[0].reshape(128, -1, 4); s[:, e] = v[1]
    return (c.reshape(128, -1), s)
def pk(c, s):
    return (np.ascontiguousarray(c), mx_ref.live(s))
def emit(q):
    return q[0], q[1]
def packed(v, rng):
    q = [mx_ref.quantize(np.ascontiguousarray(v[r])) for r in range(N)]
    return np.stack([a for a, b in q]), np.stack([mx_ref.plane(b, rng) for a, b in q])
def decode(q):
    o = []
    for b in range(4):
        e = np.zeros((128, 128, 4), np.float32); e[np.arange(128), np.arange(128), b] = 1
        o.append(mx_ref.matmul(mx_ref.quantize(e.reshape(128, 512).astype(BF)), q))
    return np.stack(o, axis=2).reshape(128, -1)
def f(rng, *shape):
    return mx_ref.flush((rng.standard_normal(shape, dtype=np.float32) * np.exp2(rng.integers(-2, 3, shape[:-1] + (1,)))).astype(BF))
def wide(rng, *shape, cols=0):
    v = rng.standard_normal(shape, dtype=np.float32) * np.exp2(rng.integers(-12, 13, shape)).astype(np.float32)
    if cols: v *= np.repeat(np.exp2(rng.integers(-cols, cols + 1, shape[:-2] + (1, shape[-1] // 4))) * (rng.random(shape[:-2] + (1, shape[-1] // 4)) > 0.0625), 4, axis=-1).astype(np.float32)
    return mx_ref.flush(v.astype(BF))
C, S, CAPP = 1024, 512, 160
def big(v, k):
    v = v.astype(np.float32) * np.float32(k)
    v[np.abs(v) < np.float32(2.0 ** -16)] = 0
    return v.astype(BF)
def names(rng, n, each):
    out, at, m = [None] * N, 0, int(n.sum())
    if not each:
        left = np.full(C, 2)
        for s in rng.permutation(N):
            out[s] = rng.permutation(np.flatnonzero(left))[:n[s]]; left[out[s]] -= 1
        return out
    a = rng.permutation(C)[:m // each]
    if each == 2: a = np.concatenate([a, rng.permutation(a)])
    for s in rng.permutation(N):
        out[s] = a[at:at + n[s]]; at += n[s]
    return out
def lists(rng, each=0, full=False, gaps=False, silent=False):
    sn, tc = np.full((N, N * CAPP), -1), np.full((N, N * CAPP), -1)
    n = np.full((N, N), CAPP) if full else rng.integers(CAPP // 4, CAPP, (N, N))
    if gaps: n[:] = CAPP - CAPP // 6
    if silent: n[:, int(rng.integers(0, N))] = 0
    for q in range(N):
        t = names(rng, n[:, q], each)
        for s in range(N): tc[q, s * CAPP + rng.permutation(CAPP)[:n[s, q]]] = t[s]
    for s in range(N):
        used = np.concatenate([tc[q, s * CAPP:s * CAPP + CAPP] >= 0 for q in range(N)])
        e = np.concatenate([rng.permutation(S), rng.integers(0, S, N * CAPP)])[:used.sum()]
        sn[s, used] = rng.permutation(e)
    return {"sn": np.stack([table(v) for v in sn]), "tc": np.stack([table(v) for v in tc])}
def setup_inputs(rng):
    c, p = packed(big(f(rng, N, 128, 4 * C), 1), rng)
    return {"wc": c, "ws": p, "gr": big(f(rng, N, 128, 4 * S), 8), **lists(rng)}
def setup_inputs_cancel(rng):
    tc, P = lists(rng, each=2, full=True, gaps=True)["tc"], S // 2
    x = rng.integers(4, 8, (128, P, 4)) * np.exp2(rng.integers(-2, 1, (128, P, 4))) * rng.choice([-1.0, 1.0], (128, P, 4)) * np.exp2(rng.integers(-2, 3, (128, P, 1)))
    h = rng.integers(0, P, (N, C))
    c, p = packed(np.stack([x[:, h[q]].reshape(128, -1) for q in range(N)]).astype(np.float32).astype(BF), rng)
    g, sn = np.zeros((N, 128, S, 4), np.float32), np.full((N, N * CAPP), -1)
    at = np.stack([rng.permutation(S) for s in range(N)])
    for s in range(N):
        g[s][:, at[s, :P]] = 8 * x
        g[s][:, at[s, P:]] = 8 * x * np.exp2(-rng.integers(21, 25, (P, 1)))
    for q in range(N):
        t = entries(tc[q]).reshape(N, CAPP)
        o = rng.permutation(np.unique(t[t >= 0]))
        late, seen = np.zeros(C, bool), np.zeros(C, bool)
        late[o[:o.size // 2]] = True
        for s in range(N):
            k = np.flatnonzero(t[s] >= 0); e = t[s][k]
            small = seen[e] != late[e]
            sn[s, q * CAPP + k] = at[s][P * small + h[q, e]]
            seen[e] = True
    return {"wc": c, "ws": p, "gr": g.reshape(N, 128, 4 * S).astype(BF), "sn": np.stack([table(v) for v in sn]), "tc": tc}
def setup_inputs_full(rng):
    return {**setup_inputs(rng), **lists(rng, full=True)}
def setup_inputs_most(rng):
    return {**setup_inputs(rng), **lists(rng, each=1, full=True, silent=True)}
def setup_inputs_spread(rng):
    d = setup_inputs(rng)
    d["wc"], d["ws"] = packed(big(wide(rng, N, 128, 4 * C, cols=8), 1), rng)
    d["gr"] = big(wide(rng, N, 128, 4 * S, cols=8), 8)
    return d
def setup_inputs_twice(rng):
    return {**setup_inputs(rng), **lists(rng, each=2, full=True)}
def check_inputs(d):
    b = []
    for r in range(N):
        a, t = entries(d["sn"][r]), entries(d["tc"][r])
        if a.min() < -1 or a.max() >= S: b.append("sn")
        sent = np.concatenate([entries(d["sn"][s])[r * CAPP:r * CAPP + CAPP] for s in range(N)])
        bad = t.min() < -1 or t.max() >= C or ((t >= 0) != (sent >= 0)).any()
        for s in range(N):
            v = t[s * CAPP:s * CAPP + CAPP]; v = v[v >= 0]
            bad = bad or len(set(v.tolist())) != v.size
        if bad or (np.unique(t[t >= 0], return_counts=True)[1] > 2).any(): b.append("tc")
    return b
def reference(wc, ws, gr, sn, tc):
    oc, osc, up = np.zeros((N, 128, 4 * C), np.uint8), np.zeros((N, 16, C), np.uint8), np.zeros((N, 1, C), np.float32)
    g = [decode(mx_ref.quantize(np.ascontiguousarray(gr[s]))).reshape(128, S, 4) for s in range(N)]
    for q in range(N):
        w = pk(wc[q], ws[q])
        v = decode(w).reshape(128, C, 4)
        for s in range(N):
            e, t = entries(sn[s])[q * CAPP:q * CAPP + CAPP], entries(tc[q])[s * CAPP:s * CAPP + CAPP]
            k = t >= 0
            v[:, t[k]] = v[:, t[k]] - g[s][:, e[k]] * np.float32(0.125)
            up[q, 0, t[k]] += 1
        named = np.flatnonzero(up[q, 0])
        new = mx_ref.quantize(np.ascontiguousarray(v.reshape(128, -1).astype(BF)))
        oc[q], osc[q] = emit(put(w, named, pick(new, named)))
    return {"oc": oc, "osc": osc, "up": up}

@@ -1,0 +1,346 @@
+from concourse.bass import DstId, RemoteDMATransfer
+from concourse.mybir import dt, AluOpType, ActivationFunctionType
+
+C, S, CAP, N = 1024, 512, 160, 4
+K = N * CAP
+H0 = 3 * CAP
+M = C // 16
+HELD = K + CAP
+DUMP = 288
+X4 = "float8_e4m3fn_x4"
+
+
+def _sb(dtype, **widths):
+    return {name: ("sbuf", [128, n], dtype) for name, n in widths.items()}
+
+
+SCRATCH = {
+    **_sb("bfloat16", ones=256, eye=128, dg=516, dm=516, zt=512, grt=4 * S, nw=4 * K),
+    **_sb(X4, ec=512, mc=512, gq=S, snd=H0, land=K + 128, wsrc=C, wi=K, par=H0, tab=HELD + C, fin=C),
+    **_sb("uint8", es=512, ms=512, gqs=S, snds=H0, lands=K + 128, wsrcs=C, wis=K, pars=H0, tabs=HELD + C, fins=C),
+    **_sb("int32", tl=42, hi=42, tcl=40, xl=32, snl=40),
+    **_sb("float32", kb=10, ke=10, jj=CAP, pcol=1, rcol=1, vals=CAP, win=DUMP + C, h2=42, u=42, lp=10, rn=512, rw=96,
+          rm=20, fw=4 * M, f1=2 * M, f2=M, c1=4 * M, c2=2 * M, c3=64, c4=64, c5=64),
+    **_sb("uint16", sno=40, wo=40, lto=10, poso=32, paro=30, fino=64),
+    "ps": ("psum", [128, 4096], "float32"),
+}
+SEMAPHORES = ["v", "s", "t", "p", "ltl", "ltc", "lx", "lsn", "lgr0", "lgr1", "lw", "ltab", "xf", "xr", "stored", "arr", "loc", "go"]
+
+
+def items(rank):
+    return [s for s in range(N) if s != rank] + [rank]
+
+
+def engines(src, dst, topo, scales):
+    e = topo.engines(src, dst)
+    return e[(topo.die(src) == topo.die(dst)) != scales::2]
+
+
+def bits(e):
+    m = 0
+    for k in e:
+        m |= 1 << k
+    return m
+
+
+def runs(where):
+    k, r = 0, []
+    while k < len(where):
+        n = 1
+        while k + n < len(where) and where[k + n] == where[k] + n:
+            n += 1
+        r.append((k, where[k], n))
+        k += n
+    return r
+
+
+def rank_program(g, core, T, topo):
+    rank = T.rank_of(core)
+    if rank is None:
+        return
+    cores = list(T.cores)
+    A, AF = AluOpType, ActivationFunctionType
+    v, sc, te, sy = g.vector, g.scalar, g.tensor, g.sync
+    queue = {"g": g, "v": v, "s": sc, "t": te, "y": sy}
+    count = {"v": 0, "s": 0, "t": 0, "p": 0, "stored": 0}
+    seen = {}
+    order = items(rank)
+    others = order[:3]
+
+    def wait(q, sem, val):
+        if seen.get((q, sem), 0) < val:
+            queue[q].wait_ge(T.sem[sem], val)
+            seen[(q, sem)] = val
+
+    def done(sem, ins):
+        ins.then_inc(T.sem[sem], 1)
+        count[sem] += 1
+        return count[sem]
+
+    def V(ins):
+        return done("v", ins)
+
+    def Sc(ins):
+        return done("s", ins)
+
+    def P(ins):
+        return done("p", ins)
+
+    def u8(ap):
+        return ap.bitcast(dt.uint8)
+
+    def u32(ap):
+        return ap.bitcast(dt.uint32)
+
+    def pick(out, at, src, lst, a, b, only="vs"):
+        n = 16 * (b - a)
+        o = T[lst][:, a:b]
+        x = y = None
+        if "v" in only:
+            x = V(v.tensor_copy(u32(T[out][:, at:at + n]), u32(T[src][:, :]).indirect(o)))
+        if "s" in only:
+            y = Sc(sc.activation(T[out + "s"][:, at:at + n], T[src + "s"][:, :].indirect(o), AF.Copy))
+        return x, y
+
+    v_xl = V(v.memset(T.xl[:, :], 0))
+    v_ones = V(v.memset(T.ones[:, :], 1.0))
+
+    def load_gr(q, h):
+        q.dma_start(T.grt[:, 1024 * h:1024 * h + 1024], T.gr[:, 1024 * h:1024 * h + 1024]).then_inc(T.sem["lgr%d" % h], 16)
+
+    def load_tl(q, lo):
+        for u in range(lo, lo + 4):
+            q.dma_start(T.tl[16 * u:16 * u + 16, 32:42], T.tc[:, 10 * (u // 2):10 * (u // 2) + 10]).then_inc(T.sem.ltl, 16)
+
+    def load_sn(q, lo):
+        for u in range(lo, lo + 4):
+            q.dma_start(T.snl[16 * u:16 * u + 16, :], T.sn[:, :]).then_inc(T.sem.lsn, 16)
+
+    load_gr(sc, 0)
+    load_tl(sc, 0)
+    load_sn(sc, 0)
+    load_tl(sy, 4)
+    wait("y", "v", v_xl)
+    for t in (1, 2, 3):
+        sy.dma_start(T.xl[32 * t:32 * t + 32, 0:16], T.tc[:, 0:32]).then_inc(T.sem.lx, 16)
+    load_gr(sy, 1)
+    load_sn(sy, 4)
+    for u in range(8):
+        sy.dma_start(T.tcl[16 * u:16 * u + 16, :], T.tc[:, :]).then_inc(T.sem.ltc, 16)
+    sy.dma_start(u8(T.wsrc[:, :]), T.wc[:, :]).then_inc(T.sem.lw, 16)
+    sy.dma_start(T.wsrcs[:, :], T.ws[:, :]).then_inc(T.sem.lw, 16)
+
+    wait("g", "v", v_ones)
+    p_eye = P(g.affine_select(T.eye[:, :], T.ones[:, 0:128], [[-1, 128]], A.is_equal, 0.0, 0, 1))
+    p_win = P(g.iota(T.win[:, DUMP:DUMP + C // 2], [[1, 8], [16, M]], HELD, 0, allow_small_or_imprecise_dtypes=True))
+    p_kb = P(g.iota(T.kb[:, :], [[16, 10]], -DUMP, 1, allow_small_or_imprecise_dtypes=True))
+    p_jj = P(g.iota(T.jj[:, :], [[1, CAP]], 0, 0, allow_small_or_imprecise_dtypes=True))
+
+    V(v.memset(T.dg[:, :], 0.0))
+    for t in range(N):
+        V(v.memset(T.pcol[32 * t:32 * t + 32, :], float(CAP * t)))
+    place = [K + CAP * t - CAP * order.index(t) for t in range(N)]
+    place[0] = place[1]
+    for t, n in ((0, 2), (2, 1), (3, 1)) if place[2] != place[3] else ((0, 2), (2, 2)):
+        v_rcol = V(v.memset(T.rcol[32 * t:32 * t + 32 * n, :], float(place[t])))
+    wait("v", "p", p_eye)
+    wait("v", "v", v_rcol)
+    v_dg = V(v.tensor_copy(T.dg[:, 3:515:4], T.eye[:, :]))
+
+    wait("s", "v", v_ones)
+    for h in range(2):
+        s_zt = Sc(sc.activation(T.zt[:, 256 * h:256 * h + 256], T.ones[:, :], AF.Copy, scale=0.0))
+    wait("s", "v", v_dg)
+    s_dm = Sc(sc.activation(T.dm[:, :], T.dg[:, :], AF.Copy, scale=-0.125))
+    wait("s", "p", p_win)
+    Sc(sc.activation(T.win[:, DUMP + C // 2:DUMP + C], T.win[:, DUMP:DUMP + C // 2], AF.Identity, bias=8.0))
+    wait("s", "p", p_kb)
+    Sc(sc.activation(T.ke[:, :], T.kb[:, :], AF.Copy, scale=1.0 / M))
+    wait("s", "p", p_jj)
+    s_con = Sc(sc.activation(T.vals[:, :], T.jj[:, :], AF.Identity, bias=T.pcol[:, 0:1]))
+
+    def constants(code, scale, tile):
+        for b in range(4):
+            V(v.quantize_mx(T[code][:, 128 * b:128 * b + 128], T[scale][:, 128 * b:128 * b + 128], T[tile][:, 3 - b:515 - b]))
+
+    wait("v", "v", v_dg)
+    constants("ec", "es", "dg")
+
+    wait("v", "lx", 48)
+    x = V(v.transpose(T.tl[:, 0:32], T.xl[:, :]))
+    wait("v", "ltl", 128)
+    wait("v", "v", x)
+    x = V(v.tensor_scalar(T.hi[:, :], T.tl[:, :], 4, None, A.logical_shift_right))
+    wait("v", "v", x)
+    v_h2 = V(v.tensor_scalar(T.h2[:, :], T.hi[:, :], -(16.0 * M - 1) / M, None, A.mult))
+
+    for h in range(2):
+        wait("v", "lgr%d" % h, 16)
+        V(v.quantize_mx(T.gq[:, 256 * h:256 * h + 256], T.gqs[:, 256 * h:256 * h + 256], T.grt[:, 1024 * h:1024 * h + 1024]))
+    wait("v", "lsn", 128)
+    v_sno = V(v.tensor_copy(T.sno[:, :], T.snl[:, :]))
+    wait("v", "v", v_h2)
+    v_u = V(v.tensor_tensor(T.u[:, :], T.tl[:, :], T.h2[:, :], A.add))
+    wait("v", "v", v_sno)
+    wait("s", "v", v_sno)
+    first = N - 1 - rank
+    for dests in ([first], [o for o in others if o != first]):
+        base = 0 if dests[0] == first else CAP
+        for k, w, n in runs(dests):
+            need = pick("snd", base + CAP * k, "gq", "sno", 10 * w, 10 * w + 10 * n)
+        for buf, to, scales in (("snd", "land", False), ("snds", "lands", True)):
+            transfers = []
+            for k, o in enumerate(dests):
+                rid, pid, _ = topo.addr(cores[o])
+                at, there = base + CAP * k, CAP * items(o).index(rank)
+                src, dst = T[buf][:, at:at + CAP], T[to][:, there:there + CAP]
+                if not scales:
+                    src, dst = u8(src), u8(dst)
+                transfers.append(RemoteDMATransfer(dst_ids=[DstId(rid=rid, pnc=pid)], dma_engine_mask=bits(engines(core, cores[o], topo, scales)),
+                                                   remote_sem=T.sem.arr, src=src, dst=dst))
+            wait("g", "s" if scales else "v", need[scales])
+            g.remote_dma_fused(transfers, local_sem=T.sem.loc)
+    g.sem_inc(T.sem.go)
+    sent = sum(len(engines(core, cores[o], topo, f)) for o in others for f in (False, True))
+    arrive = sum(len(engines(cores[o], core, topo, f)) for o in others for f in (False, True))
+
+    wait("v", "v", v_u)
+    wait("v", "s", s_con)
+    x = V(v.tensor_tensor(T.lp[:, :], T.u[:, 32:42], T.ke[:, :], A.max))
+    V(v.tensor_scalar(T.poso[:, :], T.u[:, 0:32], float(M), 0.0, A.mult, A.max))
+    wait("v", "v", x)
+    x = V(v.tensor_scalar(T.lto[:, :], T.lp[:, :], float(M), float(DUMP), A.mult, A.add))
+    wait("v", "ltc", 128)
+    v_wo = V(v.tensor_copy(T.wo[:, :], T.tcl[:, :]))
+    wait("v", "v", x)
+    v_scat = V(v.tensor_copy(T.win[:, :].indirect(T.lto[:, :]), T.vals[:, :]))
+    wait("s", "v", v_wo)
+    wait("s", "lw", 32)
+    for k, w, n in runs(others):
+        s_others = pick("wi", CAP * k, "wsrc", "wo", 10 * w, 10 * w + 10 * n, "s")[1]
+    wait("s", "v", v_scat)
+    s_rn = Sc(sc.activation(T.rn[:, :], T.win[:, DUMP:DUMP + C].indirect(T.poso[:, :]), AF.Relu, bias=T.rcol[:, 0:1], scale=-1.0))
+    wait("y", "v", v_scat)
+    for t in range(N):
+        sy.dma_start(T.fw[:, M * t:M * t + M], T.win[32 * t:32 * t + 8, DUMP:DUMP + C]).then_inc(T.sem.xf, 16)
+    wait("y", "s", s_rn)
+    for k, t in enumerate((3, 2, 1)):
+        sy.dma_start(T.rw[:, 32 * k:32 * k + 32], T.rn[32 * t:32 * t + 8, :]).then_inc(T.sem.xr, 16)
+    wait("y", "go", 1)
+    sy.dma_start(u8(T.tab[:, HELD:HELD + C]), T.wc[:, :]).then_inc(T.sem.ltab, 16)
+    sy.dma_start(T.tabs[:, HELD:HELD + C], T.ws[:, :]).then_inc(T.sem.ltab, 16)
+
+    wait("v", "lw", 32)
+    wait("v", "v", v_wo)
+    for k, w, n in runs(others):
+        v_others = pick("wi", CAP * k, "wsrc", "wo", 10 * w, 10 * w + 10 * n, "v")[0]
+    w_own = pick("wi", H0, "wsrc", "wo", 10 * rank, 10 * rank + 10)
+    wait("v", "s", s_dm)
+    constants("mc", "ms", "dm")
+    own = pick("land", H0, "gq", "sno", 10 * rank, 10 * rank + 10)
+    wait("v", "s", s_zt)
+    V(v.quantize_mx(T.land[:, K:K + 128], T.lands[:, K:K + 128], T.zt[:, :]))
+
+    t_done = {}
+
+    def product(const, half, n, mov, at, need, start, last):
+        wait("t", "v", need[0])
+        wait("t", "s", need[1])
+        for b in range(4):
+            bank = 512 * (4 * half + b)
+            t_done[(b, half)] = done("t", te.matmul_mx(T.ps[:, bank:bank + n], T[const + "c"][:, 128 * b:128 * b + 128], T[const + "s"][:, 128 * b:128 * b + 128],
+                                                       T[mov][:, at:at + n], T[mov + "s"][:, at:at + n], start, last))
+
+    product("e", 0, H0, "wi", 0, (v_others, s_others), True, False)
+    product("e", 1, CAP, "wi", H0, w_own, True, False)
+    product("m", 1, CAP, "land", H0, own, False, rank == 3)
+
+    wait("v", "xr", 48)
+    x = V(v.tensor_tensor(T.rm[:, 0:20], T.rw[:, 0:20], T.rw[:, 32:52], A.max))
+    V(v.tensor_scalar(T.paro[:, 20:30], T.rw[:, 20:30], -1.0, float(K), A.mult, A.add))
+    wait("v", "v", x)
+    x = V(v.tensor_tensor(T.rm[:, 0:10], T.rm[:, 0:10], T.rw[:, 64:74], A.max))
+    wait("v", "v", x)
+    v_paro = V(v.tensor_scalar(T.paro[:, 0:20], T.rm[:, :], -1.0, float(K), A.mult, A.add))
+    wait("s", "xf", 64)
+    s_c1 = Sc(sc.activation(T.c1[0:32, :], T.fw[0:32, :], AF.Sign, bias=0.5 - HELD))
+
+    for q in "vst":
+        wait(q, "arr", arrive)
+    wait("v", "v", v_paro)
+    wait("s", "v", v_paro)
+    wait("s", "s", own[1])
+    with_partner = [s for s in others if s != N - 1]
+    if rank != 3:
+        p_own = pick("par", 2 * CAP, "land", "paro", 10 * rank, 10 * rank + 10)
+    for k, w, n in runs(with_partner):
+        p_others = pick("par", CAP * k, "land", "paro", 10 * w, 10 * w + 10 * n)
+
+    product("m", 0, H0, "land", 0, own, False, False)
+    if rank != 3:
+        product("m", 1, CAP, "par", 2 * CAP, p_own, False, True)
+    product("m", 0, CAP * len(with_partner), "par", 0, p_others, False, True)
+
+    wait("v", "xf", 64)
+    x = V(v.tensor_tensor(T.f1[:, :], T.fw[:, 0:2 * M], T.fw[:, 2 * M:4 * M], A.min))
+    wait("v", "s", s_c1)
+    y = V(v.tensor_tensor(T.c2[0:32, :], T.c1[0:32, 0:2 * M], T.c1[0:32, 2 * M:4 * M], A.add))
+    wait("v", "v", x)
+    x = V(v.tensor_tensor(T.f2[:, :], T.f1[:, 0:M], T.f1[:, M:2 * M], A.min))
+    wait("v", "v", y)
+    v_c3 = V(v.tensor_tensor(T.c3[0:32, :], T.c2[0:32, 0:M], T.c2[0:32, M:2 * M], A.add))
+    wait("v", "v", x)
+    V(v.tensor_copy(T.fino[:, :], T.f2[:, :]))
+
+    def cast(q, b, half):
+        lo, n = (0, H0) if half == 0 else (H0, CAP)
+        wait(q, "t", t_done[(b, half)])
+        bank = 512 * (4 * half + b)
+        out, src = T.nw[:, 4 * lo + b:4 * (lo + n):4], T.ps[:, bank:bank + n]
+        return V(v.tensor_copy(out, src)) if q == "v" else Sc(sc.activation(out, src, AF.Copy))
+
+    def quantise(x, y, blocks):
+        wait("v", "v", x)
+        wait("v", "s", y)
+        for k, w, n in runs([order[b] for b in blocks]):
+            a, at, n = CAP * (blocks[0] + k), CAP * w, CAP * n
+            z = V(v.quantize_mx(T.tab[:, at:at + n], T.tabs[:, at:at + n], T.nw[:, 4 * a:4 * (a + n)]))
+        return z
+
+    cast("s", 0, 1)
+    y = cast("s", 2, 1)
+    cast("v", 1, 1)
+    x = cast("v", 3, 1)
+    cast("s", 0, 0)
+    quantise(x, y, [3])
+    cast("v", 1, 0)
+    y = cast("s", 2, 0)
+    x = cast("v", 3, 0)
+    wait("s", "v", v_c3)
+    s_c4 = Sc(sc.activation(T.c4[0:32, :], T.c3[0:32, :], AF.Identity, bias=2.0, scale=-0.5))
+    v_new = quantise(x, y, [0, 1, 2])
+
+    wait("v", "ltab", 32)
+    wait("s", "ltab", 32)
+    wait("v", "v", v_new)
+    wait("s", "v", v_new)
+    for a, b in ((0, 24), (24, 48), (48, 64)):
+        x, s_fin = pick("fin", 16 * a, "tab", "fino", a, b)
+        wait("y", "v", x)
+        sy.dma_start(T.oc[:, 64 * a:64 * b], u8(T.fin[:, 16 * a:16 * b])).then_inc(T.sem.stored, 16)
+        count["stored"] += 16
+    wait("v", "s", s_c4)
+    wait("y", "v", V(v.transpose(T.c5[0:32, :], T.c4[0:32, :])))
+    for b in range(2):
+        sy.dma_start(T.up[0:1, 512 * b:512 * b + 512], T.c5[0:32, 32 * b:32 * b + 16]).then_inc(T.sem.stored, 16)
+        count["stored"] += 16
+    wait("s", "s", s_fin)
+    wait("y", "s", s_fin)
+    for k in range(4):
+        (sc if k < 2 else sy).dma_start(T.osc[4 * k:4 * k + 4, :], T.fins[32 * k:32 * k + 4, :]).then_inc(T.sem.stored, 16)
+        count["stored"] += 16
+    wait("y", "stored", count["stored"])
+
+    wait("g", "loc", sent)
+    for sem in ("v", "s", "t", "p"):
+        wait("g", sem, count[sem])

@@ -3,11 +3,23 @@ from concourse.mybir import dt, AluOpType, ActivationFunctionType
 
 C, S, CAP, N = 1024, 512, 160, 4
 K = N * CAP
-H0 = 3 * CAP
+H = 2 * CAP
 M = C // 16
-HELD = K + CAP
 DUMP = 288
+FGATE = "scat"
+GW = 8
 X4 = "float8_e4m3fn_x4"
+PARTS = ((0, 20), (20, 44), (44, 64))
+
+ORDER = {
+    "g": "dg kb win0 jj send_near send_near_s send_far send_far_s sent",
+    "v": "dg0 zo dg1 E M turn hi zero h2 wo u lp gq0 lto gq1 scat so near wY far wX own f1 r1 r0 f2 paro f3 c2 p2 c3 p01 "
+         "castY1 castY3 castX1 qY castX3 qX c5 fin",
+    "s": "ld_tc0 ld_tl0 dm pcol ke win2 vals zero_s wY_s rn near_s wX_s far_s own_s c1 p2_s p01_s "
+         "castY0 castY2 castX0 castX2 c4 fin_s st_s0",
+    "t": "EY EX Mnear Mfar PY PX",
+    "y": "ld_tc1 ld_tl1 ld_gr0 ld_gr1 ld_sn0 ld_ws ld_sn1 ld_w sp_f sp_r0 sp_r1 ld_tab ld_tabs sp_o st_up st st_s1",
+}
 
 
 def _sb(dtype, **widths):
@@ -15,25 +27,16 @@ def _sb(dtype, **widths):
 
 
 SCRATCH = {
-    **_sb("bfloat16", ones=256, eye=128, dg=516, dm=516, zt=512, grt=4 * S, nw=4 * K),
-    **_sb(X4, ec=512, mc=512, gq=S, snd=H0, land=K + 128, wsrc=C, wi=K, par=H0, tab=HELD + C, fin=C),
-    **_sb("uint8", es=512, ms=512, gqs=S, snds=H0, lands=K + 128, wsrcs=C, wis=K, pars=H0, tabs=HELD + C, fins=C),
-    **_sb("int32", tl=42, hi=42, tcl=40, xl=32, snl=40),
-    **_sb("float32", kb=10, ke=10, jj=CAP, pcol=1, rcol=1, vals=CAP, win=DUMP + C, h2=42, u=42, lp=10, rn=512, rw=96,
-          rm=20, fw=4 * M, f1=2 * M, f2=M, c1=4 * M, c2=2 * M, c3=64, c4=64, c5=64),
-    **_sb("uint16", sno=40, wo=40, lto=10, poso=32, paro=30, fino=64),
+    **_sb("bfloat16", dg=520, dm=520, grt=4 * S, nw=4 * K, c1=4 * M, c2=2 * M, c3=M),
+    **_sb(X4, e=520, m=512, gq=S, snd=3 * CAP, land=K + 16, wsrc=C, wi=K, par=3 * CAP, tab=K + C, fin=C),
+    **_sb("uint8", es=544, ms=512, gqs=S, snds=3 * CAP, lands=K + 32, wsrcs=C, wis=K, pars=3 * CAP, tabs=K + C, fins=C),
+    **_sb("int32", tl=42, hi=26, ls=80),
+    **_sb("float32", kb=32, ke=26, jj=CAP, pcol=1, vals=CAP, win=DUMP + C, h2=26, u=26, lp=26, rn=256, rw=80,
+          fw=4 * M, f1=2 * M, f2=M, c4=M, c5=M, idle=512),
+    **_sb("uint16", so=80, lto=26, paro=30, fino=64, zo=2),
     "ps": ("psum", [128, 4096], "float32"),
 }
-SEMAPHORES = ["v", "s", "t", "p", "ltl", "ltc", "lx", "lsn", "lgr0", "lgr1", "lw", "ltab", "xf", "xr", "stored", "arr", "loc", "go"]
-
-
-def items(rank):
-    return [s for s in range(N) if s != rank] + [rank]
-
-
-def engines(src, dst, topo, scales):
-    e = topo.engines(src, dst)
-    return e[(topo.die(src) == topo.die(dst)) != scales::2]
+SEMAPHORES = ["v", "s", "t", "g", "tl", "ltc", "lsn", "lgr0", "lgr1", "lw", "lw_s", "ltab", "ltab_s", "xf", "fino", "xr", "stored", "near", "far", "loc", "locf", "go"]
 
 
 def bits(e):
@@ -41,17 +44,6 @@ def bits(e):
     for k in e:
         m |= 1 << k
     return m
-
-
-def runs(where):
-    k, r = 0, []
-    while k < len(where):
-        n = 1
-        while k + n < len(where) and where[k + n] == where[k] + n:
-            n += 1
-        r.append((k, where[k], n))
-        k += n
-    return r
 
 
 def rank_program(g, core, T, topo):
@@ -62,29 +54,19 @@ def rank_program(g, core, T, topo):
     A, AF = AluOpType, ActivationFunctionType
     v, sc, te, sy = g.vector, g.scalar, g.tensor, g.sync
     queue = {"g": g, "v": v, "s": sc, "t": te, "y": sy}
-    count = {"v": 0, "s": 0, "t": 0, "p": 0, "stored": 0}
-    seen = {}
-    order = items(rank)
-    others = order[:3]
+    far = [s for s in range(N) if topo.die(cores[s]) != topo.die(core)]
+    mate = [s for s in range(N) if s != rank and s not in far][0]
+    steps = {}
+    total = {}
+    where = {name: q for q in ORDER for name in ORDER[q].split()}
 
-    def wait(q, sem, val):
-        if seen.get((q, sem), 0) < val:
-            queue[q].wait_ge(T.sem[sem], val)
-            seen[(q, sem)] = val
+    def step(name, needs, call, sem=None, adds=16):
+        steps.setdefault(name, []).append((needs.split(), call, sem))
+        if sem:
+            total[sem] = total.get(sem, 0) + adds
 
-    def done(sem, ins):
-        ins.then_inc(T.sem[sem], 1)
-        count[sem] += 1
-        return count[sem]
-
-    def V(ins):
-        return done("v", ins)
-
-    def Sc(ins):
-        return done("s", ins)
-
-    def P(ins):
-        return done("p", ins)
+    def dma(name, needs, out, src, sem):
+        step(name, needs, lambda: queue[where[name]].dma_start(out, src).then_inc(T.sem[sem], 16), sem)
 
     def u8(ap):
         return ap.bitcast(dt.uint8)
@@ -92,255 +74,162 @@ def rank_program(g, core, T, topo):
     def u32(ap):
         return ap.bitcast(dt.uint32)
 
-    def pick(out, at, src, lst, a, b, only="vs"):
-        n = 16 * (b - a)
-        o = T[lst][:, a:b]
-        x = y = None
-        if "v" in only:
-            x = V(v.tensor_copy(u32(T[out][:, at:at + n]), u32(T[src][:, :]).indirect(o)))
-        if "s" in only:
-            y = Sc(sc.activation(T[out + "s"][:, at:at + n], T[src + "s"][:, :].indirect(o), AF.Copy))
-        return x, y
+    def pick(name, needs, out, at, src, lst, a, b, lo=0, hi=None):
+        n, o, hi = 16 * (b - a), T[lst][:, a:b], hi or T[src].shape[1]
+        step(name, needs.replace("*", ""), lambda: v.tensor_copy(u32(T[out][:, at:at + n]), u32(T[src][:, lo:hi]).indirect(o)))
+        step(name + "_s", needs.replace("*", "_s"), lambda: sc.activation(T[out + "s"][:, at:at + n], T[src + "s"][:, lo:hi].indirect(o), AF.Copy))
 
-    v_xl = V(v.memset(T.xl[:, :], 0))
-    v_ones = V(v.memset(T.ones[:, :], 1.0))
+    def quantise(name, needs, out, at, n, tile, lo):
+        step(name, needs, lambda: v.quantize_mx(T[out][:, at:at + n], T[out + "s"][:, at:at + n], T[tile][:, lo:lo + 4 * n]))
 
-    def load_gr(q, h):
-        q.dma_start(T.grt[:, 1024 * h:1024 * h + 1024], T.gr[:, 1024 * h:1024 * h + 1024]).then_inc(T.sem["lgr%d" % h], 16)
-
-    def load_tl(q, lo):
-        for u in range(lo, lo + 4):
-            q.dma_start(T.tl[16 * u:16 * u + 16, 32:42], T.tc[:, 10 * (u // 2):10 * (u // 2) + 10]).then_inc(T.sem.ltl, 16)
-
-    def load_sn(q, lo):
-        for u in range(lo, lo + 4):
-            q.dma_start(T.snl[16 * u:16 * u + 16, :], T.sn[:, :]).then_inc(T.sem.lsn, 16)
-
-    load_gr(sc, 0)
-    load_tl(sc, 0)
-    load_sn(sc, 0)
-    load_tl(sy, 4)
-    wait("y", "v", v_xl)
-    for t in (1, 2, 3):
-        sy.dma_start(T.xl[32 * t:32 * t + 32, 0:16], T.tc[:, 0:32]).then_inc(T.sem.lx, 16)
-    load_gr(sy, 1)
-    load_sn(sy, 4)
-    for u in range(8):
-        sy.dma_start(T.tcl[16 * u:16 * u + 16, :], T.tc[:, :]).then_inc(T.sem.ltc, 16)
-    sy.dma_start(u8(T.wsrc[:, :]), T.wc[:, :]).then_inc(T.sem.lw, 16)
-    sy.dma_start(T.wsrcs[:, :], T.ws[:, :]).then_inc(T.sem.lw, 16)
-
-    wait("g", "v", v_ones)
-    p_eye = P(g.affine_select(T.eye[:, :], T.ones[:, 0:128], [[-1, 128]], A.is_equal, 0.0, 0, 1))
-    p_win = P(g.iota(T.win[:, DUMP:DUMP + C // 2], [[1, 8], [16, M]], HELD, 0, allow_small_or_imprecise_dtypes=True))
-    p_kb = P(g.iota(T.kb[:, :], [[16, 10]], -DUMP, 1, allow_small_or_imprecise_dtypes=True))
-    p_jj = P(g.iota(T.jj[:, :], [[1, CAP]], 0, 0, allow_small_or_imprecise_dtypes=True))
-
-    V(v.memset(T.dg[:, :], 0.0))
-    for t in range(N):
-        V(v.memset(T.pcol[32 * t:32 * t + 32, :], float(CAP * t)))
-    place = [K + CAP * t - CAP * order.index(t) for t in range(N)]
-    place[0] = place[1]
-    for t, n in ((0, 2), (2, 1), (3, 1)) if place[2] != place[3] else ((0, 2), (2, 2)):
-        v_rcol = V(v.memset(T.rcol[32 * t:32 * t + 32 * n, :], float(place[t])))
-    wait("v", "p", p_eye)
-    wait("v", "v", v_rcol)
-    v_dg = V(v.tensor_copy(T.dg[:, 3:515:4], T.eye[:, :]))
-
-    wait("s", "v", v_ones)
-    for h in range(2):
-        s_zt = Sc(sc.activation(T.zt[:, 256 * h:256 * h + 256], T.ones[:, :], AF.Copy, scale=0.0))
-    wait("s", "v", v_dg)
-    s_dm = Sc(sc.activation(T.dm[:, :], T.dg[:, :], AF.Copy, scale=-0.125))
-    wait("s", "p", p_win)
-    Sc(sc.activation(T.win[:, DUMP + C // 2:DUMP + C], T.win[:, DUMP:DUMP + C // 2], AF.Identity, bias=8.0))
-    wait("s", "p", p_kb)
-    Sc(sc.activation(T.ke[:, :], T.kb[:, :], AF.Copy, scale=1.0 / M))
-    wait("s", "p", p_jj)
-    s_con = Sc(sc.activation(T.vals[:, :], T.jj[:, :], AF.Identity, bias=T.pcol[:, 0:1]))
-
-    def constants(code, scale, tile):
-        for b in range(4):
-            V(v.quantize_mx(T[code][:, 128 * b:128 * b + 128], T[scale][:, 128 * b:128 * b + 128], T[tile][:, 3 - b:515 - b]))
-
-    wait("v", "v", v_dg)
-    constants("ec", "es", "dg")
-
-    wait("v", "lx", 48)
-    x = V(v.transpose(T.tl[:, 0:32], T.xl[:, :]))
-    wait("v", "ltl", 128)
-    wait("v", "v", x)
-    x = V(v.tensor_scalar(T.hi[:, :], T.tl[:, :], 4, None, A.logical_shift_right))
-    wait("v", "v", x)
-    v_h2 = V(v.tensor_scalar(T.h2[:, :], T.hi[:, :], -(16.0 * M - 1) / M, None, A.mult))
-
-    for h in range(2):
-        wait("v", "lgr%d" % h, 16)
-        V(v.quantize_mx(T.gq[:, 256 * h:256 * h + 256], T.gqs[:, 256 * h:256 * h + 256], T.grt[:, 1024 * h:1024 * h + 1024]))
-    wait("v", "lsn", 128)
-    v_sno = V(v.tensor_copy(T.sno[:, :], T.snl[:, :]))
-    wait("v", "v", v_h2)
-    v_u = V(v.tensor_tensor(T.u[:, :], T.tl[:, :], T.h2[:, :], A.add))
-    wait("v", "v", v_sno)
-    wait("s", "v", v_sno)
-    first = N - 1 - rank
-    for dests in ([first], [o for o in others if o != first]):
-        base = 0 if dests[0] == first else CAP
-        for k, w, n in runs(dests):
-            need = pick("snd", base + CAP * k, "gq", "sno", 10 * w, 10 * w + 10 * n)
-        for buf, to, scales in (("snd", "land", False), ("snds", "lands", True)):
-            transfers = []
-            for k, o in enumerate(dests):
-                rid, pid, _ = topo.addr(cores[o])
-                at, there = base + CAP * k, CAP * items(o).index(rank)
-                src, dst = T[buf][:, at:at + CAP], T[to][:, there:there + CAP]
-                if not scales:
-                    src, dst = u8(src), u8(dst)
-                transfers.append(RemoteDMATransfer(dst_ids=[DstId(rid=rid, pnc=pid)], dma_engine_mask=bits(engines(core, cores[o], topo, scales)),
-                                                   remote_sem=T.sem.arr, src=src, dst=dst))
-            wait("g", "s" if scales else "v", need[scales])
-            g.remote_dma_fused(transfers, local_sem=T.sem.loc)
-    g.sem_inc(T.sem.go)
-    sent = sum(len(engines(core, cores[o], topo, f)) for o in others for f in (False, True))
-    arrive = sum(len(engines(cores[o], core, topo, f)) for o in others for f in (False, True))
-
-    wait("v", "v", v_u)
-    wait("v", "s", s_con)
-    x = V(v.tensor_tensor(T.lp[:, :], T.u[:, 32:42], T.ke[:, :], A.max))
-    V(v.tensor_scalar(T.poso[:, :], T.u[:, 0:32], float(M), 0.0, A.mult, A.max))
-    wait("v", "v", x)
-    x = V(v.tensor_scalar(T.lto[:, :], T.lp[:, :], float(M), float(DUMP), A.mult, A.add))
-    wait("v", "ltc", 128)
-    v_wo = V(v.tensor_copy(T.wo[:, :], T.tcl[:, :]))
-    wait("v", "v", x)
-    v_scat = V(v.tensor_copy(T.win[:, :].indirect(T.lto[:, :]), T.vals[:, :]))
-    wait("s", "v", v_wo)
-    wait("s", "lw", 32)
-    for k, w, n in runs(others):
-        s_others = pick("wi", CAP * k, "wsrc", "wo", 10 * w, 10 * w + 10 * n, "s")[1]
-    wait("s", "v", v_scat)
-    s_rn = Sc(sc.activation(T.rn[:, :], T.win[:, DUMP:DUMP + C].indirect(T.poso[:, :]), AF.Relu, bias=T.rcol[:, 0:1], scale=-1.0))
-    wait("y", "v", v_scat)
-    for t in range(N):
-        sy.dma_start(T.fw[:, M * t:M * t + M], T.win[32 * t:32 * t + 8, DUMP:DUMP + C]).then_inc(T.sem.xf, 16)
-    wait("y", "s", s_rn)
-    for k, t in enumerate((3, 2, 1)):
-        sy.dma_start(T.rw[:, 32 * k:32 * k + 32], T.rn[32 * t:32 * t + 8, :]).then_inc(T.sem.xr, 16)
-    wait("y", "go", 1)
-    sy.dma_start(u8(T.tab[:, HELD:HELD + C]), T.wc[:, :]).then_inc(T.sem.ltab, 16)
-    sy.dma_start(T.tabs[:, HELD:HELD + C], T.ws[:, :]).then_inc(T.sem.ltab, 16)
-
-    wait("v", "lw", 32)
-    wait("v", "v", v_wo)
-    for k, w, n in runs(others):
-        v_others = pick("wi", CAP * k, "wsrc", "wo", 10 * w, 10 * w + 10 * n, "v")[0]
-    w_own = pick("wi", H0, "wsrc", "wo", 10 * rank, 10 * rank + 10)
-    wait("v", "s", s_dm)
-    constants("mc", "ms", "dm")
-    own = pick("land", H0, "gq", "sno", 10 * rank, 10 * rank + 10)
-    wait("v", "s", s_zt)
-    V(v.quantize_mx(T.land[:, K:K + 128], T.lands[:, K:K + 128], T.zt[:, :]))
-
-    t_done = {}
-
-    def product(const, half, n, mov, at, need, start, last):
-        wait("t", "v", need[0])
-        wait("t", "s", need[1])
+    def products(name, needs, const, half, n, mov, start, last):
+        at = H * half
         for b in range(4):
             bank = 512 * (4 * half + b)
-            t_done[(b, half)] = done("t", te.matmul_mx(T.ps[:, bank:bank + n], T[const + "c"][:, 128 * b:128 * b + 128], T[const + "s"][:, 128 * b:128 * b + 128],
-                                                       T[mov][:, at:at + n], T[mov + "s"][:, at:at + n], start, last))
+            step(name, needs, lambda b=b, bank=bank: te.matmul_mx(T.ps[:, bank:bank + n], T[const][:, 128 * b:128 * b + 128], T[const + "s"][:, 128 * b:128 * b + 128],
+                                                                  T[mov][:, at:at + n], T[mov + "s"][:, at:at + n], start, last))
 
-    product("e", 0, H0, "wi", 0, (v_others, s_others), True, False)
-    product("e", 1, CAP, "wi", H0, w_own, True, False)
-    product("m", 1, CAP, "land", H0, own, False, rank == 3)
+    for h in range(2):
+        dma("ld_gr%d" % h, "", T.grt[:, 1024 * h:1024 * h + 1024], T.gr[:, 1024 * h:1024 * h + 1024], "lgr%d" % h)
+    for u in range(8):
+        dma("ld_sn%d" % (u // 4), "", T.ls[16 * u:16 * u + 16, 0:40], T.sn[:, :], "lsn")
+        dma("ld_tc%d" % (u // 4), "", T.ls[16 * u:16 * u + 16, 40:80], T.tc[:, :], "ltc")
+        if "tl" not in where:
+            dma("ld_tl%d" % (u // 4), "", T.tl[16 * u:16 * u + 16, 32:42], T.tc[:, 10 * (u // 2):10 * (u // 2) + 10], "tl")
+    for t in range(N):
+        if "tl" in where:
+            step("tl", "ltc", lambda t=t: v.tensor_copy(T.tl[32 * t:32 * t + 32, 32:42], T.ls[32 * t:32 * t + 32, 40 + 10 * t:50 + 10 * t]))
+    dma("ld_w", "", u8(T.wsrc[:, :]), T.wc[:, :], "lw")
+    dma("ld_ws", "", T.wsrcs[:, :], T.ws[:, :], "lw_s")
+    step("sent", "", lambda: g.sem_inc(T.sem.go), "go", 1)
+    dma("ld_tabs", "locf go", T.tabs[:, K:K + C], T.ws[:, :], "ltab_s")
+    dma("ld_tab", "locf go", u8(T.tab[:, K:K + C]), T.wc[:, :], "ltab")
 
-    wait("v", "xr", 48)
-    x = V(v.tensor_tensor(T.rm[:, 0:20], T.rw[:, 0:20], T.rw[:, 32:52], A.max))
-    V(v.tensor_scalar(T.paro[:, 20:30], T.rw[:, 20:30], -1.0, float(K), A.mult, A.add))
-    wait("v", "v", x)
-    x = V(v.tensor_tensor(T.rm[:, 0:10], T.rm[:, 0:10], T.rw[:, 64:74], A.max))
-    wait("v", "v", x)
-    v_paro = V(v.tensor_scalar(T.paro[:, 0:20], T.rm[:, :], -1.0, float(K), A.mult, A.add))
-    wait("s", "xf", 64)
-    s_c1 = Sc(sc.activation(T.c1[0:32, :], T.fw[0:32, :], AF.Sign, bias=0.5 - HELD))
+    step("dg0", "", lambda: v.memset(T.dg[:, 3:520:4], 0.0))
+    for b in range(3):
+        step("dg1", "", lambda b=b: v.memset(T.dg[:, b:520:4], 0.0))
+    step("dg", "dg0", lambda: g.affine_select(T.dg[:, 3:515:4], T.dg[:, 3:515:4], [[-1, 128]], A.not_equal, 1.0, 0, 1))
+    if where["dm"] == "s":
+        step("dm", "dg dg1", lambda: sc.activation(T.dm[:, :], T.dg[:, :], AF.Copy, scale=-0.125))
+    else:
+        step("dm0", "", lambda: v.memset(T.dm[:, :], 0.0))
+        step("dm", "dm0", lambda: g.affine_select(T.dm[:, 3:515:4], T.dm[:, 3:515:4], [[-1, 128]], A.not_equal, -0.125, 0, 1))
+    for b in range(4):
+        quantise("E", "dg dg1", "e", 128 * b, 128 + 2 * (b == 3), "dg", 3 - b)
+        quantise("M", "dm", "m", 128 * b, 128, "dm", 3 - b)
+    step("zo", "", lambda: v.memset(T.zo[:, :], 0))
+    pick("zero", "E zo", "land", K, "e", "zo", 0, 1, 512, 514)
+    step("kb", "", lambda: g.iota(T.kb[:, :], [[-DUMP, 2], [16, 16]], 0, 1, allow_small_or_imprecise_dtypes=True))
+    step("ke", "kb", lambda: sc.activation(T.ke[:, :], T.kb[:, 0:26], AF.Relu, scale=-1.0 / M))
+    step("win0", "", lambda: g.iota(T.win[:, DUMP:DUMP + GW * M], [[1, GW], [16, M]], K, 0, allow_small_or_imprecise_dtypes=True))
+    step("win2", "win0", lambda: sc.activation(T.win[:, DUMP + GW * M:DUMP + C], T.win[:, DUMP:DUMP + C - GW * M], AF.Identity, bias=float(GW)))
+    for t in range(N):
+        if where["pcol"] == "v":
+            step("pcol", "", lambda t=t: v.memset(T.pcol[32 * t:32 * t + 32, :], float(CAP * t)))
+        else:
+            step("pcol", "dg1", lambda t=t: sc.activation(T.pcol[32 * t:32 * t + 32, :], T.dg[32 * t:32 * t + 32, 516:517], AF.Identity, bias=float(CAP * t)))
+    step("jj", "", lambda: g.iota(T.jj[:, :], [[1, CAP]], 0, 0, allow_small_or_imprecise_dtypes=True))
+    step("vals", "jj pcol", lambda: sc.activation(T.vals[:, :], T.jj[:, :], AF.Identity, bias=T.pcol[:, 0:1]))
 
-    for q in "vst":
-        wait(q, "arr", arrive)
-    wait("v", "v", v_paro)
-    wait("s", "v", v_paro)
-    wait("s", "s", own[1])
-    with_partner = [s for s in others if s != N - 1]
-    if rank != 3:
-        p_own = pick("par", 2 * CAP, "land", "paro", 10 * rank, 10 * rank + 10)
-    for k, w, n in runs(with_partner):
-        p_others = pick("par", CAP * k, "land", "paro", 10 * w, 10 * w + 10 * n)
+    for h in range(2):
+        quantise("gq%d" % h, "lgr%d" % h, "gq", 256 * h, 256, "grt", 1024 * h)
+    step("so", "lsn", lambda: v.tensor_copy(T.so[:, 0:40], T.ls[:, 0:40]))
+    step("wo", "ltc", lambda: v.tensor_copy(T.so[:, 40:80], T.ls[:, 40:80]))
+    for name, dests, base in (("near", [mate], 0), ("far", far, CAP)):
+        pick(name, "gq0 gq1 so", "snd", base, "gq", "so", 10 * dests[0], 10 * dests[-1] + 10)
+        for buf, to, tail in (("snd", "land", ""), ("snds", "lands", "_s")):
+            transfers, adds, loc = [], 0, "locf" if name + tail == "near" else "loc"
+            for k, o in enumerate(dests):
+                rid, pid, _ = topo.addr(cores[o])
+                src, dst = T[buf][:, base + CAP * k:base + CAP * (k + 1)], T[to][:, CAP * rank:CAP * (rank + 1)]
+                if not tail:
+                    src, dst = u8(src), u8(dst)
+                e = topo.engines(core, cores[o])[(k + len(tail) // 2) % 2::2]
+                transfers.append(RemoteDMATransfer(dst_ids=[DstId(rid=rid, pnc=pid)], dma_engine_mask=bits(e), remote_sem=T.sem[name], src=src, dst=dst))
+                adds += len(e)
+            step("send_" + name + tail, name + tail, lambda x=transfers, y=loc: g.remote_dma_fused(x, local_sem=T.sem[y]), loc, adds)
+    total["@near"] = len(topo.engines(cores[mate], core))
+    total["@far"] = sum(len(topo.engines(cores[o], core)) for o in far)
+    pick("own", "gq0 gq1 so", "land", CAP * rank, "gq", "so", 10 * rank, 10 * rank + 10)
 
-    product("m", 0, H0, "land", 0, own, False, False)
-    if rank != 3:
-        product("m", 1, CAP, "par", 2 * CAP, p_own, False, True)
-    product("m", 0, CAP * len(with_partner), "par", 0, p_others, False, True)
-
-    wait("v", "xf", 64)
-    x = V(v.tensor_tensor(T.f1[:, :], T.fw[:, 0:2 * M], T.fw[:, 2 * M:4 * M], A.min))
-    wait("v", "s", s_c1)
-    y = V(v.tensor_tensor(T.c2[0:32, :], T.c1[0:32, 0:2 * M], T.c1[0:32, 2 * M:4 * M], A.add))
-    wait("v", "v", x)
-    x = V(v.tensor_tensor(T.f2[:, :], T.f1[:, 0:M], T.f1[:, M:2 * M], A.min))
-    wait("v", "v", y)
-    v_c3 = V(v.tensor_tensor(T.c3[0:32, :], T.c2[0:32, 0:M], T.c2[0:32, M:2 * M], A.add))
-    wait("v", "v", x)
-    V(v.tensor_copy(T.fino[:, :], T.f2[:, :]))
-
-    def cast(q, b, half):
-        lo, n = (0, H0) if half == 0 else (H0, CAP)
-        wait(q, "t", t_done[(b, half)])
-        bank = 512 * (4 * half + b)
-        out, src = T.nw[:, 4 * lo + b:4 * (lo + n):4], T.ps[:, bank:bank + n]
-        return V(v.tensor_copy(out, src)) if q == "v" else Sc(sc.activation(out, src, AF.Copy))
-
-    def quantise(x, y, blocks):
-        wait("v", "v", x)
-        wait("v", "s", y)
-        for k, w, n in runs([order[b] for b in blocks]):
-            a, at, n = CAP * (blocks[0] + k), CAP * w, CAP * n
-            z = V(v.quantize_mx(T.tab[:, at:at + n], T.tabs[:, at:at + n], T.nw[:, 4 * a:4 * (a + n)]))
-        return z
-
-    cast("s", 0, 1)
-    y = cast("s", 2, 1)
-    cast("v", 1, 1)
-    x = cast("v", 3, 1)
-    cast("s", 0, 0)
-    quantise(x, y, [3])
-    cast("v", 1, 0)
-    y = cast("s", 2, 0)
-    x = cast("v", 3, 0)
-    wait("s", "v", v_c3)
-    s_c4 = Sc(sc.activation(T.c4[0:32, :], T.c3[0:32, :], AF.Identity, bias=2.0, scale=-0.5))
-    v_new = quantise(x, y, [0, 1, 2])
-
-    wait("v", "ltab", 32)
-    wait("s", "ltab", 32)
-    wait("v", "v", v_new)
-    wait("s", "v", v_new)
-    for a, b in ((0, 24), (24, 48), (48, 64)):
-        x, s_fin = pick("fin", 16 * a, "tab", "fino", a, b)
-        wait("y", "v", x)
-        sy.dma_start(T.oc[:, 64 * a:64 * b], u8(T.fin[:, 16 * a:16 * b])).then_inc(T.sem.stored, 16)
-        count["stored"] += 16
-    wait("v", "s", s_c4)
-    wait("y", "v", V(v.transpose(T.c5[0:32, :], T.c4[0:32, :])))
+    step("idle", "", lambda: v.memset(T.idle[:, :], 0.0))
+    step("turn", "ltc", lambda: v.transpose(T.tl[:, 0:32], T.ls[:, 40:72]))
+    step("hi", "turn tl", lambda: v.tensor_scalar(T.hi[:, :], T.tl[:, 16:42], 4, None, A.logical_shift_right))
+    step("h2", "hi", lambda: v.tensor_scalar(T.h2[:, :], T.hi[:, :], (16.0 * M - 1) / M, None, A.mult))
+    step("u", "h2", lambda: v.tensor_tensor(T.u[:, :], T.h2[:, :], T.tl[:, 16:42], A.subtract))
+    step("lp", "u ke", lambda: v.tensor_tensor(T.lp[:, :], T.u[:, :], T.ke[:, :], A.min))
+    step("lto", "lp", lambda: v.tensor_scalar(T.lto[:, :], T.lp[:, :], -float(M), float(DUMP), A.mult, A.add))
+    step("scat", "lto vals win2", lambda: v.tensor_copy(T.win[:, :].indirect(T.lto[:, 16:26]), T.vals[:, :]))
+    step("rn", "scat", lambda: sc.activation(T.rn[:, :], T.win[:, :].indirect(T.lto[:, 0:16]), AF.Relu, bias=float(K), scale=-1.0))
+    for u in (7, 6, 4, 5, 2):
+        c = 32 * (3 - u // 2) + 16 * (u % 2)
+        dma("sp_r%d" % (u < 5), "rn", T.rw[:, c:c + 16], T.rn[16 * u:16 * u + 8, :], "xr")
+    for t in range(N):
+        dma("sp_f", FGATE, T.fw[0:32, M * t:M * t + M], T.win[32 * t:32 * t + 2, DUMP:DUMP + C], "xf")
+    step("r1", "xr", lambda: v.tensor_tensor(T.rw[:, 0:20], T.rw[:, 0:20], T.rw[:, 32:52], A.max))
+    step("r0", "r1", lambda: v.tensor_tensor(T.rw[:, 0:10], T.rw[:, 0:10], T.rw[:, 64:74], A.max))
+    step("paro", "r0", lambda: v.tensor_scalar(T.paro[:, :], T.rw[:, 0:30], -1.0, float(K - CAP), A.mult, A.add))
+    step("f1", "xf", lambda: v.tensor_tensor(T.f1[0:32, :], T.fw[0:32, 0:2 * M], T.fw[0:32, 2 * M:4 * M], A.min))
+    step("f2", "f1", lambda: v.tensor_tensor(T.f2[0:32, :], T.f1[0:32, 0:M], T.f1[0:32, M:2 * M], A.min))
+    step("f3", "f2", lambda: v.tensor_copy(T.fino[0:32, :], T.f2[0:32, :]))
+    for t in range(1, N):
+        dma("sp_o", "f3", T.fino[32 * t:32 * t + 32, :], T.fino[0:32, :], "fino")
+    step("c1", "xf", lambda: sc.activation(T.c1[0:32, :], T.fw[0:32, :], AF.Sign, bias=0.5 - K))
+    step("c2", "c1", lambda: v.tensor_tensor(T.c2[0:32, :], T.c1[0:32, 0:2 * M], T.c1[0:32, 2 * M:4 * M], A.add))
+    step("c3", "c2", lambda: v.tensor_tensor(T.c3[0:32, :], T.c2[0:32, 0:M], T.c2[0:32, M:2 * M], A.add))
+    step("c4", "c3", lambda: sc.activation(T.c4[0:32, :], T.c3[0:32, :], AF.Identity, bias=2.0, scale=-0.5))
+    step("c5", "c4", lambda: v.transpose(T.c5[0:32, :], T.c4[0:32, :]))
     for b in range(2):
-        sy.dma_start(T.up[0:1, 512 * b:512 * b + 512], T.c5[0:32, 32 * b:32 * b + 16]).then_inc(T.sem.stored, 16)
-        count["stored"] += 16
-    wait("s", "s", s_fin)
-    wait("y", "s", s_fin)
-    for k in range(4):
-        (sc if k < 2 else sy).dma_start(T.osc[4 * k:4 * k + 4, :], T.fins[32 * k:32 * k + 4, :]).then_inc(T.sem.stored, 16)
-        count["stored"] += 16
-    wait("y", "stored", count["stored"])
+        dma("st_up", "c5", T.up[0:1, 512 * b:512 * b + 512], T.c5[0:32, 32 * b:32 * b + 16], "stored")
 
-    wait("g", "loc", sent)
-    for sem in ("v", "s", "t", "p"):
-        wait("g", sem, count[sem])
+    pick("p2", "@near @far own* zero* paro", "par", H, "land", "paro", 20, 30, CAP, K + 2)
+    pick("p01", "@near @far own* zero* paro", "par", 0, "land", "paro", 0, 20, CAP, K + 2)
+    for half, name in enumerate("XY"):
+        lo = H * half
+        pick("w" + name, "lw* wo", "wi", lo, "wsrc", "so", 40 + 20 * half, 60 + 20 * half)
+        products("E" + name, "E w%s w%s_s" % (name, name), "e", half, H, "wi", True, False)
+        if CAP * far[0] == lo:
+            products("Mfar", "M @far", "m", half, H, "land", False, False)
+        else:
+            products("Mnear", "M own own_s @near", "m", half, H, "land", False, False)
+        products("P" + name, "p2 p2_s" if half else "p01 p01_s", "m", half, CAP if half else H, "par", False, True)
+        for b in range(4):
+            bank, cast = 512 * (4 * half + b), "cast%s%d" % (name, b)
+            out, src = T.nw[:, 4 * lo + b:4 * (lo + H):4], T.ps[:, bank:bank + H]
+            step(cast, "P%s.%d" % (name, b),
+                 (lambda o=out, s=src: v.tensor_copy(o, s)) if where[cast] == "v" else (lambda o=out, s=src: sc.activation(o, s, AF.Copy)))
+        quantise("q" + name, " ".join("cast%s%d" % (name, b) for b in range(4)), "tab", lo, H, "nw", 4 * lo)
+
+    for k, (a, b) in enumerate(PARTS):
+        step("fin", "ltab qX qY fino", lambda a=a, b=b: v.tensor_copy(u32(T.fin[:, 16 * a:16 * b]), u32(T.tab[:, :]).indirect(T.fino[:, a:b])))
+        dma("st", "fin.%d" % k, T.oc[:, 64 * a:64 * b], u8(T.fin[:, 16 * a:16 * b]), "stored")
+    step("fin_s", "ltab_s qX qY fino", lambda: sc.activation(T.fins[:, :], T.tabs[:, :].indirect(T.fino[:, :]), AF.Copy))
+    for k in range(4):
+        dma("st_s%d" % (k // 2), "fin_s", T.osc[4 * k:4 * k + 4, :], T.fins[32 * k:32 * k + 4, :], "stored")
+
+    count, met = {q: 0 for q in ORDER}, {}
+    for q in ORDER:
+        for name in ORDER[q].split():
+            for k, (needs, call, sem) in enumerate(steps[name]):
+                if not sem:
+                    count[q] += 1
+                    met[name] = met["%s.%d" % (name, k)] = (q, count[q])
+    met.update({name: (name.strip("@"), n) for name, n in total.items()})
+    for q in ORDER:
+        seen, issued = {}, 0
+        last = {"y": ["stored"], "g": ["loc", "locf"]}.get(q, [])
+        for needs, call, sem in [x for name in ORDER[q].split() for x in steps[name]] + [(last, None, None)]:
+            waits = {}
+            for need in needs:
+                waits[met[need][0]] = max(waits.get(met[need][0], 0), met[need][1])
+            for s, val in waits.items():
+                if seen.get(s, 0) < val:
+                    seen[s] = max(val, issued - 1) if s == q else val
+                    queue[q].wait_ge(T.sem[s], seen[s])
+            if call:
+                ins = call()
+                if not sem:
+                    ins.then_inc(T.sem[q], 1)
+                    issued += 1
+    for q in "vstg":
+        g.wait_ge(T.sem[q], count[q])

from concourse.bass import DstId, RemoteDMATransfer
from concourse.mybir import dt, AluOpType, ActivationFunctionType

C, S, CAP, N = 1024, 512, 160, 4
K = N * CAP
H = 2 * CAP
M = C // 16
DUMP = 288
FGATE = "scat"
GW = 8
X4 = "float8_e4m3fn_x4"
PARTS = ((0, 20), (20, 44), (44, 64))

ORDER = {
    "g": "dg kb win0 jj send_near send_near_s send_far send_far_s sent",
    "v": "dg0 zo dg1 E M turn hi zero h2 wo u lp gq0 lto gq1 scat so near wY far wX own f1 r1 r0 f2 paro f3 c2 p2 c3 p01 "
         "castY1 castY3 castX1 qY castX3 qX c5 fin",
    "s": "ld_tc0 ld_tl0 dm pcol ke win2 vals zero_s wY_s rn near_s wX_s far_s own_s c1 p2_s p01_s "
         "castY0 castY2 castX0 castX2 c4 fin_s st_s0",
    "t": "EY EX Mnear Mfar PY PX",
    "y": "ld_tc1 ld_tl1 ld_gr0 ld_gr1 ld_sn0 ld_ws ld_sn1 ld_w sp_f sp_r0 sp_r1 ld_tab ld_tabs sp_o st_up st st_s1",
}


def _sb(dtype, **widths):
    return {name: ("sbuf", [128, n], dtype) for name, n in widths.items()}


SCRATCH = {
    **_sb("bfloat16", dg=520, dm=520, grt=4 * S, nw=4 * K, c1=4 * M, c2=2 * M, c3=M),
    **_sb(X4, e=520, m=512, gq=S, snd=3 * CAP, land=K + 16, wsrc=C, wi=K, par=3 * CAP, tab=K + C, fin=C),
    **_sb("uint8", es=544, ms=512, gqs=S, snds=3 * CAP, lands=K + 32, wsrcs=C, wis=K, pars=3 * CAP, tabs=K + C, fins=C),
    **_sb("int32", tl=42, hi=26, ls=80),
    **_sb("float32", kb=32, ke=26, jj=CAP, pcol=1, vals=CAP, win=DUMP + C, h2=26, u=26, lp=26, rn=256, rw=80,
          fw=4 * M, f1=2 * M, f2=M, c4=M, c5=M, idle=512),
    **_sb("uint16", so=80, lto=26, paro=30, fino=64, zo=2),
    "ps": ("psum", [128, 4096], "float32"),
}
SEMAPHORES = ["v", "s", "t", "g", "tl", "ltc", "lsn", "lgr0", "lgr1", "lw", "lw_s", "ltab", "ltab_s", "xf", "fino", "xr", "stored", "near", "far", "loc", "locf", "go"]


def bits(e):
    m = 0
    for k in e:
        m |= 1 << k
    return m


def rank_program(g, core, T, topo):
    rank = T.rank_of(core)
    if rank is None:
        return
    cores = list(T.cores)
    A, AF = AluOpType, ActivationFunctionType
    v, sc, te, sy = g.vector, g.scalar, g.tensor, g.sync
    queue = {"g": g, "v": v, "s": sc, "t": te, "y": sy}
    far = [s for s in range(N) if topo.die(cores[s]) != topo.die(core)]
    mate = [s for s in range(N) if s != rank and s not in far][0]
    steps = {}
    total = {}
    where = {name: q for q in ORDER for name in ORDER[q].split()}

    def step(name, needs, call, sem=None, adds=16):
        steps.setdefault(name, []).append((needs.split(), call, sem))
        if sem:
            total[sem] = total.get(sem, 0) + adds

    def dma(name, needs, out, src, sem):
        step(name, needs, lambda: queue[where[name]].dma_start(out, src).then_inc(T.sem[sem], 16), sem)

    def u8(ap):
        return ap.bitcast(dt.uint8)

    def u32(ap):
        return ap.bitcast(dt.uint32)

    def pick(name, needs, out, at, src, lst, a, b, lo=0, hi=None):
        n, o, hi = 16 * (b - a), T[lst][:, a:b], hi or T[src].shape[1]
        step(name, needs.replace("*", ""), lambda: v.tensor_copy(u32(T[out][:, at:at + n]), u32(T[src][:, lo:hi]).indirect(o)))
        step(name + "_s", needs.replace("*", "_s"), lambda: sc.activation(T[out + "s"][:, at:at + n], T[src + "s"][:, lo:hi].indirect(o), AF.Copy))

    def quantise(name, needs, out, at, n, tile, lo):
        step(name, needs, lambda: v.quantize_mx(T[out][:, at:at + n], T[out + "s"][:, at:at + n], T[tile][:, lo:lo + 4 * n]))

    def products(name, needs, const, half, n, mov, start, last):
        at = H * half
        for b in range(4):
            bank = 512 * (4 * half + b)
            step(name, needs, lambda b=b, bank=bank: te.matmul_mx(T.ps[:, bank:bank + n], T[const][:, 128 * b:128 * b + 128], T[const + "s"][:, 128 * b:128 * b + 128],
                                                                  T[mov][:, at:at + n], T[mov + "s"][:, at:at + n], start, last))

    for h in range(2):
        dma("ld_gr%d" % h, "", T.grt[:, 1024 * h:1024 * h + 1024], T.gr[:, 1024 * h:1024 * h + 1024], "lgr%d" % h)
    for u in range(8):
        dma("ld_sn%d" % (u // 4), "", T.ls[16 * u:16 * u + 16, 0:40], T.sn[:, :], "lsn")
        dma("ld_tc%d" % (u // 4), "", T.ls[16 * u:16 * u + 16, 40:80], T.tc[:, :], "ltc")
        if "tl" not in where:
            dma("ld_tl%d" % (u // 4), "", T.tl[16 * u:16 * u + 16, 32:42], T.tc[:, 10 * (u // 2):10 * (u // 2) + 10], "tl")
    for t in range(N):
        if "tl" in where:
            step("tl", "ltc", lambda t=t: v.tensor_copy(T.tl[32 * t:32 * t + 32, 32:42], T.ls[32 * t:32 * t + 32, 40 + 10 * t:50 + 10 * t]))
    dma("ld_w", "", u8(T.wsrc[:, :]), T.wc[:, :], "lw")
    dma("ld_ws", "", T.wsrcs[:, :], T.ws[:, :], "lw_s")
    step("sent", "", lambda: g.sem_inc(T.sem.go), "go", 1)
    dma("ld_tabs", "locf go", T.tabs[:, K:K + C], T.ws[:, :], "ltab_s")
    dma("ld_tab", "locf go", u8(T.tab[:, K:K + C]), T.wc[:, :], "ltab")

    step("dg0", "", lambda: v.memset(T.dg[:, 3:520:4], 0.0))
    for b in range(3):
        step("dg1", "", lambda b=b: v.memset(T.dg[:, b:520:4], 0.0))
    step("dg", "dg0", lambda: g.affine_select(T.dg[:, 3:515:4], T.dg[:, 3:515:4], [[-1, 128]], A.not_equal, 1.0, 0, 1))
    if where["dm"] == "s":
        step("dm", "dg dg1", lambda: sc.activation(T.dm[:, :], T.dg[:, :], AF.Copy, scale=-0.125))
    else:
        step("dm0", "", lambda: v.memset(T.dm[:, :], 0.0))
        step("dm", "dm0", lambda: g.affine_select(T.dm[:, 3:515:4], T.dm[:, 3:515:4], [[-1, 128]], A.not_equal, -0.125, 0, 1))
    for b in range(4):
        quantise("E", "dg dg1", "e", 128 * b, 128 + 2 * (b == 3), "dg", 3 - b)
        quantise("M", "dm", "m", 128 * b, 128, "dm", 3 - b)
    step("zo", "", lambda: v.memset(T.zo[:, :], 0))
    pick("zero", "E zo", "land", K, "e", "zo", 0, 1, 512, 514)
    step("kb", "", lambda: g.iota(T.kb[:, :], [[-DUMP, 2], [16, 16]], 0, 1, allow_small_or_imprecise_dtypes=True))
    step("ke", "kb", lambda: sc.activation(T.ke[:, :], T.kb[:, 0:26], AF.Relu, scale=-1.0 / M))
    step("win0", "", lambda: g.iota(T.win[:, DUMP:DUMP + GW * M], [[1, GW], [16, M]], K, 0, allow_small_or_imprecise_dtypes=True))
    step("win2", "win0", lambda: sc.activation(T.win[:, DUMP + GW * M:DUMP + C], T.win[:, DUMP:DUMP + C - GW * M], AF.Identity, bias=float(GW)))
    for t in range(N):
        if where["pcol"] == "v":
            step("pcol", "", lambda t=t: v.memset(T.pcol[32 * t:32 * t + 32, :], float(CAP * t)))
        else:
            step("pcol", "dg1", lambda t=t: sc.activation(T.pcol[32 * t:32 * t + 32, :], T.dg[32 * t:32 * t + 32, 516:517], AF.Identity, bias=float(CAP * t)))
    step("jj", "", lambda: g.iota(T.jj[:, :], [[1, CAP]], 0, 0, allow_small_or_imprecise_dtypes=True))
    step("vals", "jj pcol", lambda: sc.activation(T.vals[:, :], T.jj[:, :], AF.Identity, bias=T.pcol[:, 0:1]))

    for h in range(2):
        quantise("gq%d" % h, "lgr%d" % h, "gq", 256 * h, 256, "grt", 1024 * h)
    step("so", "lsn", lambda: v.tensor_copy(T.so[:, 0:40], T.ls[:, 0:40]))
    step("wo", "ltc", lambda: v.tensor_copy(T.so[:, 40:80], T.ls[:, 40:80]))
    for name, dests, base in (("near", [mate], 0), ("far", far, CAP)):
        pick(name, "gq0 gq1 so", "snd", base, "gq", "so", 10 * dests[0], 10 * dests[-1] + 10)
        for buf, to, tail in (("snd", "land", ""), ("snds", "lands", "_s")):
            transfers, adds, loc = [], 0, "locf" if name + tail == "near" else "loc"
            for k, o in enumerate(dests):
                rid, pid, _ = topo.addr(cores[o])
                src, dst = T[buf][:, base + CAP * k:base + CAP * (k + 1)], T[to][:, CAP * rank:CAP * (rank + 1)]
                if not tail:
                    src, dst = u8(src), u8(dst)
                e = topo.engines(core, cores[o])[(k + len(tail) // 2) % 2::2]
                transfers.append(RemoteDMATransfer(dst_ids=[DstId(rid=rid, pnc=pid)], dma_engine_mask=bits(e), remote_sem=T.sem[name], src=src, dst=dst))
                adds += len(e)
            step("send_" + name + tail, name + tail, lambda x=transfers, y=loc: g.remote_dma_fused(x, local_sem=T.sem[y]), loc, adds)
    total["@near"] = len(topo.engines(cores[mate], core))
    total["@far"] = sum(len(topo.engines(cores[o], core)) for o in far)
    pick("own", "gq0 gq1 so", "land", CAP * rank, "gq", "so", 10 * rank, 10 * rank + 10)

    step("idle", "", lambda: v.memset(T.idle[:, :], 0.0))
    step("turn", "ltc", lambda: v.transpose(T.tl[:, 0:32], T.ls[:, 40:72]))
    step("hi", "turn tl", lambda: v.tensor_scalar(T.hi[:, :], T.tl[:, 16:42], 4, None, A.logical_shift_right))
    step("h2", "hi", lambda: v.tensor_scalar(T.h2[:, :], T.hi[:, :], (16.0 * M - 1) / M, None, A.mult))
    step("u", "h2", lambda: v.tensor_tensor(T.u[:, :], T.h2[:, :], T.tl[:, 16:42], A.subtract))
    step("lp", "u ke", lambda: v.tensor_tensor(T.lp[:, :], T.u[:, :], T.ke[:, :], A.min))
    step("lto", "lp", lambda: v.tensor_scalar(T.lto[:, :], T.lp[:, :], -float(M), float(DUMP), A.mult, A.add))
    step("scat", "lto vals win2", lambda: v.tensor_copy(T.win[:, :].indirect(T.lto[:, 16:26]), T.vals[:, :]))
    step("rn", "scat", lambda: sc.activation(T.rn[:, :], T.win[:, :].indirect(T.lto[:, 0:16]), AF.Relu, bias=float(K), scale=-1.0))
    for u in (7, 6, 4, 5, 2):
        c = 32 * (3 - u // 2) + 16 * (u % 2)
        dma("sp_r%d" % (u < 5), "rn", T.rw[:, c:c + 16], T.rn[16 * u:16 * u + 8, :], "xr")
    for t in range(N):
        dma("sp_f", FGATE, T.fw[0:32, M * t:M * t + M], T.win[32 * t:32 * t + 2, DUMP:DUMP + C], "xf")
    step("r1", "xr", lambda: v.tensor_tensor(T.rw[:, 0:20], T.rw[:, 0:20], T.rw[:, 32:52], A.max))
    step("r0", "r1", lambda: v.tensor_tensor(T.rw[:, 0:10], T.rw[:, 0:10], T.rw[:, 64:74], A.max))
    step("paro", "r0", lambda: v.tensor_scalar(T.paro[:, :], T.rw[:, 0:30], -1.0, float(K - CAP), A.mult, A.add))
    step("f1", "xf", lambda: v.tensor_tensor(T.f1[0:32, :], T.fw[0:32, 0:2 * M], T.fw[0:32, 2 * M:4 * M], A.min))
    step("f2", "f1", lambda: v.tensor_tensor(T.f2[0:32, :], T.f1[0:32, 0:M], T.f1[0:32, M:2 * M], A.min))
    step("f3", "f2", lambda: v.tensor_copy(T.fino[0:32, :], T.f2[0:32, :]))
    for t in range(1, N):
        dma("sp_o", "f3", T.fino[32 * t:32 * t + 32, :], T.fino[0:32, :], "fino")
    step("c1", "xf", lambda: sc.activation(T.c1[0:32, :], T.fw[0:32, :], AF.Sign, bias=0.5 - K))
    step("c2", "c1", lambda: v.tensor_tensor(T.c2[0:32, :], T.c1[0:32, 0:2 * M], T.c1[0:32, 2 * M:4 * M], A.add))
    step("c3", "c2", lambda: v.tensor_tensor(T.c3[0:32, :], T.c2[0:32, 0:M], T.c2[0:32, M:2 * M], A.add))
    step("c4", "c3", lambda: sc.activation(T.c4[0:32, :], T.c3[0:32, :], AF.Identity, bias=2.0, scale=-0.5))
    step("c5", "c4", lambda: v.transpose(T.c5[0:32, :], T.c4[0:32, :]))
    for b in range(2):
        dma("st_up", "c5", T.up[0:1, 512 * b:512 * b + 512], T.c5[0:32, 32 * b:32 * b + 16], "stored")

    pick("p2", "@near @far own* zero* paro", "par", H, "land", "paro", 20, 30, CAP, K + 2)
    pick("p01", "@near @far own* zero* paro", "par", 0, "land", "paro", 0, 20, CAP, K + 2)
    for half, name in enumerate("XY"):
        lo = H * half
        pick("w" + name, "lw* wo", "wi", lo, "wsrc", "so", 40 + 20 * half, 60 + 20 * half)
        products("E" + name, "E w%s w%s_s" % (name, name), "e", half, H, "wi", True, False)
        if CAP * far[0] == lo:
            products("Mfar", "M @far", "m", half, H, "land", False, False)
        else:
            products("Mnear", "M own own_s @near", "m", half, H, "land", False, False)
        products("P" + name, "p2 p2_s" if half else "p01 p01_s", "m", half, CAP if half else H, "par", False, True)
        for b in range(4):
            bank, cast = 512 * (4 * half + b), "cast%s%d" % (name, b)
            out, src = T.nw[:, 4 * lo + b:4 * (lo + H):4], T.ps[:, bank:bank + H]
            step(cast, "P%s.%d" % (name, b),
                 (lambda o=out, s=src: v.tensor_copy(o, s)) if where[cast] == "v" else (lambda o=out, s=src: sc.activation(o, s, AF.Copy)))
        quantise("q" + name, " ".join("cast%s%d" % (name, b) for b in range(4)), "tab", lo, H, "nw", 4 * lo)

    for k, (a, b) in enumerate(PARTS):
        step("fin", "ltab qX qY fino", lambda a=a, b=b: v.tensor_copy(u32(T.fin[:, 16 * a:16 * b]), u32(T.tab[:, :]).indirect(T.fino[:, a:b])))
        dma("st", "fin.%d" % k, T.oc[:, 64 * a:64 * b], u8(T.fin[:, 16 * a:16 * b]), "stored")
    step("fin_s", "ltab_s qX qY fino", lambda: sc.activation(T.fins[:, :], T.tabs[:, :].indirect(T.fino[:, :]), AF.Copy))
    for k in range(4):
        dma("st_s%d" % (k // 2), "fin_s", T.osc[4 * k:4 * k + 4, :], T.fins[32 * k:32 * k + 4, :], "stored")

    count, met = {q: 0 for q in ORDER}, {}
    for q in ORDER:
        for name in ORDER[q].split():
            for k, (needs, call, sem) in enumerate(steps[name]):
                if not sem:
                    count[q] += 1
                    met[name] = met["%s.%d" % (name, k)] = (q, count[q])
    met.update({name: (name.strip("@"), n) for name, n in total.items()})
    for q in ORDER:
        seen, issued = {}, 0
        last = {"y": ["stored"], "g": ["loc", "locf"]}.get(q, [])
        for needs, call, sem in [x for name in ORDER[q].split() for x in steps[name]] + [(last, None, None)]:
            waits = {}
            for need in needs:
                waits[met[need][0]] = max(waits.get(met[need][0], 0), met[need][1])
            for s, val in waits.items():
                if seen.get(s, 0) < val:
                    seen[s] = max(val, issued - 1) if s == q else val
                    queue[q].wait_ge(T.sem[s], seen[s])
            if call:
                ins = call()
                if not sem:
                    ins.then_inc(T.sem[q], 1)
                    issued += 1
    for q in "vstg":
        g.wait_ge(T.sem[q], count[q])
